import numpy as np
import ml_dtypes


def mxq(x, axis, fmt="e4m3"):
    dtype, down = {"e4m3": (ml_dtypes.float8_e4m3fn, 7), "e5m2": (ml_dtypes.float8_e5m2, 14)}[fmt]
    v = np.moveaxis(np.asarray(x, np.float32).astype(ml_dtypes.bfloat16).astype(np.float64), axis, -1)
    blocks = v.reshape(v.shape[:-1] + (-1, 32))
    amax = np.abs(blocks).max(-1, keepdims=True)
    byte = np.maximum(np.where(amax > 0, np.frexp(amax)[1] - 1 + 127, 0) - down, 1)
    scale = np.exp2(byte - 127.0)
    codes = (blocks / scale).astype(np.float32).astype(dtype).astype(np.float64)
    return np.moveaxis((codes * scale).reshape(v.shape), -1, axis)


WIDE = False


def mx_kscale(k):
    if not WIDE:
        return np.ones(k)
    levels = np.array([10, -10, 5, -5, 0])
    if k % 512:
        return np.exp2(np.random.permutation(np.resize(levels, k // 32))).repeat(32)
    a = np.empty((k // 512, 16))
    for p in range(k // 512):
        a[p, :8] = np.random.permutation(np.resize(levels, 8))
        for g in range(8):
            far = levels[np.abs(levels - a[p, g]) >= 10]
            a[p, g + 8] = far[np.random.randint(len(far))]
    return np.exp2(a.ravel()).repeat(32)


def f64(x):
    return np.asarray(x).astype(np.float64)


def striped(idx):
    return np.tile(np.asarray(idx).reshape(-1, 16).T, (8, 1)).astype(np.uint16)


def unstriped(offs):
    return offs[:16].T.reshape(-1).astype(np.int64)


G, K, T, D, M = 512, 4, 4096, 512, 256


def setup_inputs():
    n = np.random.standard_normal
    s = mx_kscale(D)[:, None]
    grid = lambda x: np.round(x * 32) / 32
    x = grid(n((D, T))) * s
    idx = np.random.randint(0, T, (G, K))
    part = np.random.randint(1, 128 // K, (G, K)) / 64.0
    return {
        "xT": x.astype(np.float32),
        "w": (n((D, M)) / np.sqrt(D) / s).astype(np.float32),
        "part": np.tile(part.reshape(-1), (128, 1)).astype(np.float32),
        "offs": striped(idx.reshape(-1)),
    }


def reference(xT, w, part, offs):
    x = f64(xT)[:, unstriped(offs)]
    y = mxq(f64(w), 0, "e4m3").T @ mxq((x * f64(part)[:1]).reshape(D, G, K).sum(-1), 0, "e4m3")
    return y

@@ -1,0 +1,130 @@
+from contextlib import ExitStack
+
+import concourse.mybir as mybir
+from concourse.masks import make_identity
+
+F32 = mybir.dt.float32
+BF16 = mybir.dt.bfloat16
+U32 = mybir.dt.uint32
+U16 = mybir.dt.uint16
+U8 = mybir.dt.uint8
+FP8X4 = mybir.dt.float8_e4m3fn_x4
+MULT = mybir.AluOpType.mult
+
+P = 128
+T = 4096
+D = 512
+M = 256
+G = 512
+K = 4
+E = G * K
+PACK = 4
+FLOPS = 2 * D * M * G
+
+PIECES = (1024, 1024, 1024, 512)
+
+
+def tile_attend_grid_kernel(tc, xT, w, part, offs, out):
+    nc = tc.nc
+    x_planes = xT.rearrange("(p t) c -> p t c", t=PACK)
+    with ExitStack() as ctx:
+        held = ctx.enter_context(tc.tile_pool(name="held", bufs=1))
+        ring = ctx.enter_context(tc.tile_pool(name="ring", bufs=4))
+        psum = ctx.enter_context(tc.psum_pool(name="psum", bufs=1))
+
+        offsets = held.tile([P, E // 16], U16, name="offsets")
+        nc.sync.dma_start(offsets[:], offs)
+        part_col = held.tile([P, E // P], F32, name="part_col")
+        nc.sync.dma_start(part_col[:], part[0:1, :].rearrange("o (q i) -> (o q) i", i=E // P))
+        planes = []
+        for t in range(PACK):
+            plane = held.tile([P, T], F32, name=f"plane{t}")
+            for h in range(2):
+                cols = slice(h * T // 2, (h + 1) * T // 2)
+                nc.sync.dma_start(plane[:, cols], x_planes[:, t, cols])
+            planes.append(plane)
+        w_raw = held.tile([P, PACK, M], F32, name="w_raw")
+        nc.sync.dma_start(w_raw[:], w.rearrange("(p t) m -> p t m", t=PACK))
+
+        ident = held.tile([P, P], F32, name="ident")
+        make_identity(nc, ident[:])
+
+        part_rep = held.tile([P, E], F32, name="part_rep")
+        part_view = part_rep[:].rearrange("p (q i) -> p q i", i=E // P)
+        for b in range(4):
+            bank = psum.tile([P, 4, P], F32, name=f"part_bank{b}", tag=f"back{b}")
+            for i in range(4):
+                col = part_col[:, 4 * b + i : 4 * b + i + 1]
+                nc.tensor.transpose(bank[:, i, :], col.to_broadcast([P, P]), ident[:])
+            src = bank[:].rearrange("p i q -> p q i")
+            dst = part_view[:, :, 4 * b : 4 * b + 4]
+            if b % 2 == 0:
+                nc.vector.tensor_copy(dst, src)
+            else:
+                nc.scalar.copy(dst, src)
+
+        sums = [psum.tile([P, PACK, P], F32, name=f"sums{k}", tag=f"fore{k}") for k in range(4)]
+        backs = [psum.tile([P, PACK, P], F32, name=f"backs{k}", tag=f"back{k}") for k in range(4)]
+
+        for t in range(PACK):
+            piece = PIECES[t]
+            for e0 in range(0, E, piece):
+                prod = ring.tile([P, piece], F32, name=f"prod_{piece}")
+                nc.vector.tensor_tensor(
+                    prod[:],
+                    planes[t][:].indirect(offsets[:, e0 // 16 : (e0 + piece) // 16]),
+                    part_rep[:, e0 : e0 + piece],
+                    MULT,
+                )
+                by_corner = prod[:].rearrange("p (g j) -> p j g", j=K)
+                for c in range(piece // 512):
+                    k = e0 // 512 + c
+                    for j in range(K):
+                        nc.tensor.matmul(
+                            sums[k][:, t, :],
+                            by_corner[:, j, c * P : (c + 1) * P],
+                            ident[:],
+                            start=(j == 0),
+                            stop=(j == K - 1),
+                            is_transpose=True,
+                        )
+                    turned = ring.tile([P, P], F32, name="turned")
+                    nc.scalar.copy(turned[:], sums[k][:, t, :])
+                    nc.tensor.transpose(backs[k][:, t, :], turned[:], ident[:])
+
+        w_grouped = held.tile([P, M, PACK], BF16, name="w_grouped", align_bytes=64)
+        nc.scalar.copy(w_grouped[:], w_raw[:].rearrange("p t m -> p m t"))
+        w_codes = held.tile([P, M], U32, name="w_codes", align_bytes=64)
+        w_scales = held.tile([P, M], U8, name="w_scales", align_bytes=64)
+        nc.vector.quantize_mx(
+            out=w_codes[:].bitcast(FP8X4), scales=w_scales[:], in_=w_grouped[:].rearrange("p m t -> p (m t)")
+        )
+
+        for k in range(4):
+            grouped = held.tile([P, P, PACK], BF16, name=f"grouped{k}", align_bytes=64)
+            codes = held.tile([P, P], U32, name=f"codes{k}", align_bytes=64)
+            scales = held.tile([P, P], U8, name=f"scales{k}", align_bytes=64)
+            src = backs[k][:].rearrange("p t g -> p g t")
+            if k < 3:
+                nc.scalar.copy(grouped[:], src)
+            else:
+                nc.scalar.copy(grouped[:, :64, :], src[:, :64, :])
+                nc.vector.tensor_copy(grouped[:, 64:, :], src[:, 64:, :])
+            nc.vector.quantize_mx(
+                out=codes[:].bitcast(FP8X4), scales=scales[:], in_=grouped[:].rearrange("p g t -> p (g t)")
+            )
+            acc = psum.tile([P, 2, P], F32, name=f"acc{k}", tag=f"fore{k}")
+            for m in range(2):
+                cols = slice(m * P, (m + 1) * P)
+                nc.tensor.matmul_mx(
+                    out=acc[:, m, :],
+                    lhsT=w_codes[:, cols].bitcast(FP8X4),
+                    lhsT_scale=w_scales[:, cols],
+                    rhs=codes[:].bitcast(FP8X4),
+                    rhs_scale=scales[:],
+                    start=True,
+                    stop=True,
+                )
+            result = held.tile([P, 2, P], F32, name=f"result{k}")
+            nc.scalar.copy(result[:], acc[:])
+            nc.sync.dma_start(out[:, k * P : (k + 1) * P].rearrange("(m p) g -> p m g", m=2), result[:])

@@ -10,6 +10,7 @@ U16 = mybir.dt.uint16
 U8 = mybir.dt.uint8
 FP8X4 = mybir.dt.float8_e4m3fn_x4
 MULT = mybir.AluOpType.mult
+ADD = mybir.AluOpType.add
 
 P = 128
 T = 4096
@@ -21,7 +22,7 @@ E = G * K
 PACK = 4
 FLOPS = 2 * D * M * G
 
-PIECES = (1024, 1024, 1024, 512)
+PIECES = (2048, 2048, 1024, 512)
 
 
 def tile_attend_grid_kernel(tc, xT, w, part, offs, out):
@@ -30,12 +31,13 @@ def tile_attend_grid_kernel(tc, xT, w, part, offs, out):
     with ExitStack() as ctx:
         held = ctx.enter_context(tc.tile_pool(name="held", bufs=1))
         ring = ctx.enter_context(tc.tile_pool(name="ring", bufs=4))
+        wide = ctx.enter_context(tc.tile_pool(name="wide", bufs=2))
         psum = ctx.enter_context(tc.psum_pool(name="psum", bufs=1))
 
         offsets = held.tile([P, E // 16], U16, name="offsets")
         nc.sync.dma_start(offsets[:], offs)
         part_col = held.tile([P, E // P], F32, name="part_col")
-        nc.sync.dma_start(part_col[:], part[0:1, :].rearrange("o (q i) -> (o q) i", i=E // P))
+        nc.scalar.dma_start(part_col[:], part[0:1, :].rearrange("o (q i) -> (o q) i", i=E // P))
         planes = []
         for t in range(PACK):
             plane = held.tile([P, T], F32, name=f"plane{t}")
@@ -66,53 +68,55 @@ def tile_attend_grid_kernel(tc, xT, w, part, offs, out):
         sums = [psum.tile([P, PACK, P], F32, name=f"sums{k}", tag=f"fore{k}") for k in range(4)]
         backs = [psum.tile([P, PACK, P], F32, name=f"backs{k}", tag=f"back{k}") for k in range(4)]
 
+        w_grouped = held.tile([P, M, PACK], BF16, name="w_grouped", align_bytes=64)
+        w_codes = held.tile([P, M], U32, name="w_codes", align_bytes=64)
+        w_scales = held.tile([P, M], U8, name="w_scales", align_bytes=64)
+        last_e = held.tile([P, PACK, P], F32, name="last_e")
+
+        def sum_corners(relaid, t, k):
+            for j in range(K):
+                nc.tensor.matmul(
+                    sums[k][:, t, :], relaid[:, j, :], ident[:], start=(j == 0), stop=(j == K - 1), is_transpose=True
+                )
+            turned = ring.tile([P, P], F32, name="turned")
+            nc.scalar.copy(turned[:], sums[k][:, t, :])
+            nc.tensor.transpose(backs[k][:, t, :], turned[:], ident[:])
+
         for t in range(PACK):
             piece = PIECES[t]
             for e0 in range(0, E, piece):
-                prod = ring.tile([P, piece], F32, name=f"prod_{piece}")
+                prod = wide.tile([P, piece], F32, name=f"prod_{piece}")
                 nc.vector.tensor_tensor(
                     prod[:],
                     planes[t][:].indirect(offsets[:, e0 // 16 : (e0 + piece) // 16]),
                     part_rep[:, e0 : e0 + piece],
                     MULT,
                 )
-                by_corner = prod[:].rearrange("p (g j) -> p j g", j=K)
                 for c in range(piece // 512):
                     k = e0 // 512 + c
-                    for j in range(K):
-                        nc.tensor.matmul(
-                            sums[k][:, t, :],
-                            by_corner[:, j, c * P : (c + 1) * P],
-                            ident[:],
-                            start=(j == 0),
-                            stop=(j == K - 1),
-                            is_transpose=True,
-                        )
-                    turned = ring.tile([P, P], F32, name="turned")
-                    nc.scalar.copy(turned[:], sums[k][:, t, :])
-                    nc.tensor.transpose(backs[k][:, t, :], turned[:], ident[:])
+                    if t == 3 and k == 3:
+                        continue
+                    relaid = ring.tile([P, K, P], F32, name="relaid")
+                    nc.scalar.copy(
+                        relaid[:].rearrange("p j g -> p g j"),
+                        prod[:, c * 512 : (c + 1) * 512].rearrange("p (g j) -> p g j", j=K),
+                    )
+                    sum_corners(relaid, t, k)
+            if t == 2:
+                nc.scalar.copy(last_e[:, 0:3, :], backs[3][:, 0:3, :])
+                nc.scalar.copy(w_grouped[:], w_raw[:].rearrange("p t m -> p m t"))
 
-        w_grouped = held.tile([P, M, PACK], BF16, name="w_grouped", align_bytes=64)
-        nc.scalar.copy(w_grouped[:], w_raw[:].rearrange("p t m -> p m t"))
-        w_codes = held.tile([P, M], U32, name="w_codes", align_bytes=64)
-        w_scales = held.tile([P, M], U8, name="w_scales", align_bytes=64)
-        nc.vector.quantize_mx(
-            out=w_codes[:].bitcast(FP8X4), scales=w_scales[:], in_=w_grouped[:].rearrange("p m t -> p (m t)")
-        )
+        grouped = [held.tile([P, P, PACK], BF16, name=f"grouped{k}", align_bytes=64) for k in range(4)]
 
-        for k in range(4):
-            grouped = held.tile([P, P, PACK], BF16, name=f"grouped{k}", align_bytes=64)
+        def quantize(k):
             codes = held.tile([P, P], U32, name=f"codes{k}", align_bytes=64)
             scales = held.tile([P, P], U8, name=f"scales{k}", align_bytes=64)
-            src = backs[k][:].rearrange("p t g -> p g t")
-            if k < 3:
-                nc.scalar.copy(grouped[:], src)
-            else:
-                nc.scalar.copy(grouped[:, :64, :], src[:, :64, :])
-                nc.vector.tensor_copy(grouped[:, 64:, :], src[:, 64:, :])
             nc.vector.quantize_mx(
-                out=codes[:].bitcast(FP8X4), scales=scales[:], in_=grouped[:].rearrange("p g t -> p (g t)")
+                out=codes[:].bitcast(FP8X4), scales=scales[:], in_=grouped[k][:].rearrange("p g t -> p (g t)")
             )
+            return codes, scales
+
+        def multiply(k, codes, scales):
             acc = psum.tile([P, 2, P], F32, name=f"acc{k}", tag=f"fore{k}")
             for m in range(2):
                 cols = slice(m * P, (m + 1) * P)
@@ -126,5 +130,28 @@ def tile_attend_grid_kernel(tc, xT, w, part, offs, out):
                     stop=True,
                 )
             result = held.tile([P, 2, P], F32, name=f"result{k}")
-            nc.scalar.copy(result[:], acc[:])
+            if k < 3:
+                nc.scalar.copy(result[:], acc[:])
+            else:
+                nc.scalar.copy(result[:, 0, :], acc[:, 0, :])
+                nc.vector.tensor_copy(result[:, 1, :], acc[:, 1, :])
             nc.sync.dma_start(out[:, k * P : (k + 1) * P].rearrange("(m p) g -> p m g", m=2), result[:])
+
+        halves = held.tile([P, P, 2], F32, name="halves")
+        by_pair = prod[:].rearrange("p (g h j) -> p h g j", h=2, j=2)
+        nc.vector.tensor_tensor(halves[:], by_pair[:, 0], by_pair[:, 1], ADD)
+        nc.vector.quantize_mx(
+            out=w_codes[:].bitcast(FP8X4), scales=w_scales[:], in_=w_grouped[:].rearrange("p m t -> p (m t)")
+        )
+        for k in range(3):
+            nc.scalar.copy(grouped[k][:], backs[k][:].rearrange("p t g -> p g t"))
+        q0 = quantize(0)
+        nc.vector.tensor_tensor(last_e[:, 3, :], halves[:, :, 0], halves[:, :, 1], ADD)
+        q1 = quantize(1)
+        nc.vector.tensor_copy(grouped[3][:], last_e[:].rearrange("p t g -> p g t"))
+        q2 = quantize(2)
+        q3 = quantize(3)
+        multiply(0, q0[0], q0[1])
+        multiply(1, q1[0], q1[1])
+        multiply(2, q2[0], q2[1])
+        multiply(3, q3[0], q3[1])

@@ -31,7 +31,7 @@ def tile_attend_grid_kernel(tc, xT, w, part, offs, out):
     with ExitStack() as ctx:
         held = ctx.enter_context(tc.tile_pool(name="held", bufs=1))
         ring = ctx.enter_context(tc.tile_pool(name="ring", bufs=4))
-        wide = ctx.enter_context(tc.tile_pool(name="wide", bufs=2))
+        wide = ctx.enter_context(tc.tile_pool(name="wide", bufs=3))
         psum = ctx.enter_context(tc.psum_pool(name="psum", bufs=1))
 
         offsets = held.tile([P, E // 16], U16, name="offsets")
@@ -96,24 +96,20 @@ def tile_attend_grid_kernel(tc, xT, w, part, offs, out):
                     k = e0 // 512 + c
                     if t == 3 and k == 3:
                         continue
-                    relaid = ring.tile([P, K, P], F32, name="relaid")
-                    nc.scalar.copy(
-                        relaid[:].rearrange("p j g -> p g j"),
-                        prod[:, c * 512 : (c + 1) * 512].rearrange("p (g j) -> p g j", j=K),
-                    )
-                    sum_corners(relaid, t, k)
+                    sum_corners(prod[:, c * 512 : (c + 1) * 512].rearrange("p (g j) -> p j g", j=K), t, k)
             if t == 2:
                 nc.scalar.copy(last_e[:, 0:3, :], backs[3][:, 0:3, :])
                 nc.scalar.copy(w_grouped[:], w_raw[:].rearrange("p t m -> p m t"))
 
-        grouped = [held.tile([P, P, PACK], BF16, name=f"grouped{k}", align_bytes=64) for k in range(4)]
+        pair = held.tile([P, 2, P, PACK], BF16, name="pair", align_bytes=64)
+        third = held.tile([P, P, PACK], BF16, name="third", align_bytes=64)
+        fourth = held.tile([P, P, PACK], BF16, name="fourth", align_bytes=64)
 
-        def quantize(k):
-            codes = held.tile([P, P], U32, name=f"codes{k}", align_bytes=64)
-            scales = held.tile([P, P], U8, name=f"scales{k}", align_bytes=64)
-            nc.vector.quantize_mx(
-                out=codes[:].bitcast(FP8X4), scales=scales[:], in_=grouped[k][:].rearrange("p g t -> p (g t)")
-            )
+        def quantize(flat, name):
+            n = flat.shape[1] // PACK
+            codes = held.tile([P, n], U32, name=f"codes{name}", align_bytes=64)
+            scales = held.tile([P, n], U8, name=f"scales{name}", align_bytes=64)
+            nc.vector.quantize_mx(out=codes[:].bitcast(FP8X4), scales=scales[:], in_=flat)
             return codes, scales
 
         def multiply(k, codes, scales):
@@ -124,14 +120,16 @@ def tile_attend_grid_kernel(tc, xT, w, part, offs, out):
                     out=acc[:, m, :],
                     lhsT=w_codes[:, cols].bitcast(FP8X4),
                     lhsT_scale=w_scales[:, cols],
-                    rhs=codes[:].bitcast(FP8X4),
-                    rhs_scale=scales[:],
+                    rhs=codes.bitcast(FP8X4),
+                    rhs_scale=scales,
                     start=True,
                     stop=True,
                 )
             result = held.tile([P, 2, P], F32, name=f"result{k}")
-            if k < 3:
+            if k < 2:
                 nc.scalar.copy(result[:], acc[:])
+            elif k == 2:
+                nc.vector.tensor_copy(result[:], acc[:])
             else:
                 nc.scalar.copy(result[:, 0, :], acc[:, 0, :])
                 nc.vector.tensor_copy(result[:, 1, :], acc[:, 1, :])
@@ -143,15 +141,17 @@ def tile_attend_grid_kernel(tc, xT, w, part, offs, out):
         nc.vector.quantize_mx(
             out=w_codes[:].bitcast(FP8X4), scales=w_scales[:], in_=w_grouped[:].rearrange("p m t -> p (m t)")
         )
-        for k in range(3):
-            nc.scalar.copy(grouped[k][:], backs[k][:].rearrange("p t g -> p g t"))
-        q0 = quantize(0)
+        for k in range(2):
+            nc.scalar.copy(pair[:, k], backs[k][:].rearrange("p t g -> p g t"))
+        nc.scalar.copy(third[:], backs[2][:].rearrange("p t g -> p g t"))
         nc.vector.tensor_tensor(last_e[:, 3, :], halves[:, :, 0], halves[:, :, 1], ADD)
-        q1 = quantize(1)
-        nc.vector.tensor_copy(grouped[3][:], last_e[:].rearrange("p t g -> p g t"))
-        q2 = quantize(2)
-        q3 = quantize(3)
-        multiply(0, q0[0], q0[1])
-        multiply(1, q1[0], q1[1])
-        multiply(2, q2[0], q2[1])
-        multiply(3, q3[0], q3[1])
+        c01, s01 = quantize(pair[:].rearrange("p k g t -> p (k g t)"), "01")
+        last_view = last_e[:].rearrange("p t g -> p g t")
+        nc.scalar.copy(fourth[:, :64], last_view[:, :64])
+        nc.vector.tensor_copy(fourth[:, 64:], last_view[:, 64:])
+        c2, s2 = quantize(third[:].rearrange("p g t -> p (g t)"), "2")
+        c3, s3 = quantize(fourth[:].rearrange("p g t -> p (g t)"), "3")
+        multiply(0, c01[:, :P], s01[:, :P])
+        multiply(1, c01[:, P:], s01[:, P:])
+        multiply(2, c2[:], s2[:])
+        multiply(3, c3[:], s3[:])

@@ -22,7 +22,7 @@ E = G * K
 PACK = 4
 FLOPS = 2 * D * M * G
 
-PIECES = (2048, 2048, 1024, 512)
+PIECES = ((1024, 1024), (1024, 1024), (1024, 512, 512), (512, 512, 512, 512))
 
 
 def tile_attend_grid_kernel(tc, xT, w, part, offs, out):
@@ -72,6 +72,8 @@ def tile_attend_grid_kernel(tc, xT, w, part, offs, out):
         w_codes = held.tile([P, M], U32, name="w_codes", align_bytes=64)
         w_scales = held.tile([P, M], U8, name="w_scales", align_bytes=64)
         last_e = held.tile([P, PACK, P], F32, name="last_e")
+        nc.gpsimd.memset(last_e[:, 3, :], 0.0)
+        fourth = held.tile([P, P, PACK], BF16, name="fourth", align_bytes=64)
 
         def sum_corners(relaid, t, k):
             for j in range(K):
@@ -80,11 +82,18 @@ def tile_attend_grid_kernel(tc, xT, w, part, offs, out):
                 )
             turned = ring.tile([P, P], F32, name="turned")
             nc.scalar.copy(turned[:], sums[k][:, t, :])
-            nc.tensor.transpose(backs[k][:, t, :], turned[:], ident[:])
+            return turned, t, k
 
+        def turn_back(turned, t, k):
+            nc.tensor.transpose(backs[k][:, t, :], turned[:], ident[:])
+            if (t, k) == (2, 3):
+                nc.scalar.copy(last_e[:, 0:3, :], backs[3][:, 0:3, :])
+                nc.scalar.copy(fourth[:], last_e[:].rearrange("p t g -> p g t"))
+
+        waiting = []
         for t in range(PACK):
-            piece = PIECES[t]
-            for e0 in range(0, E, piece):
+            e0 = 0
+            for piece in PIECES[t]:
                 prod = wide.tile([P, piece], F32, name=f"prod_{piece}")
                 nc.vector.tensor_tensor(
                     prod[:],
@@ -96,14 +105,18 @@ def tile_attend_grid_kernel(tc, xT, w, part, offs, out):
                     k = e0 // 512 + c
                     if t == 3 and k == 3:
                         continue
-                    sum_corners(prod[:, c * 512 : (c + 1) * 512].rearrange("p (g j) -> p j g", j=K), t, k)
-            if t == 2:
-                nc.scalar.copy(last_e[:, 0:3, :], backs[3][:, 0:3, :])
-                nc.scalar.copy(w_grouped[:], w_raw[:].rearrange("p t m -> p m t"))
+                    waiting.append(
+                        sum_corners(prod[:, c * 512 : (c + 1) * 512].rearrange("p (g j) -> p j g", j=K), t, k)
+                    )
+                    if len(waiting) > 1:
+                        turn_back(*waiting.pop(0))
+                    if (t, k) == (3, 0):
+                        nc.scalar.copy(w_grouped[:], w_raw[:].rearrange("p t m -> p m t"))
+                e0 += piece
+        turn_back(*waiting.pop(0))
 
         pair = held.tile([P, 2, P, PACK], BF16, name="pair", align_bytes=64)
         third = held.tile([P, P, PACK], BF16, name="third", align_bytes=64)
-        fourth = held.tile([P, P, PACK], BF16, name="fourth", align_bytes=64)
 
         def quantize(flat, name):
             n = flat.shape[1] // PACK
@@ -128,30 +141,27 @@ def tile_attend_grid_kernel(tc, xT, w, part, offs, out):
             result = held.tile([P, 2, P], F32, name=f"result{k}")
             if k < 2:
                 nc.scalar.copy(result[:], acc[:])
-            elif k == 2:
+            elif k == 3:
                 nc.vector.tensor_copy(result[:], acc[:])
             else:
                 nc.scalar.copy(result[:, 0, :], acc[:, 0, :])
                 nc.vector.tensor_copy(result[:, 1, :], acc[:, 1, :])
             nc.sync.dma_start(out[:, k * P : (k + 1) * P].rearrange("(m p) g -> p m g", m=2), result[:])
 
-        halves = held.tile([P, P, 2], F32, name="halves")
-        by_pair = prod[:].rearrange("p (g h j) -> p h g j", h=2, j=2)
-        nc.vector.tensor_tensor(halves[:], by_pair[:, 0], by_pair[:, 1], ADD)
+        with nc.allow_low_precision(reason="the float32 sum of four products is rounded to bfloat16 once, on the way out"):
+            nc.vector.tensor_reduce(
+                fourth[:, :, 3], prod[:].rearrange("p (g j) -> p g j", j=K), mybir.AxisListType.X, ADD
+            )
         nc.vector.quantize_mx(
             out=w_codes[:].bitcast(FP8X4), scales=w_scales[:], in_=w_grouped[:].rearrange("p m t -> p (m t)")
         )
         for k in range(2):
             nc.scalar.copy(pair[:, k], backs[k][:].rearrange("p t g -> p g t"))
         nc.scalar.copy(third[:], backs[2][:].rearrange("p t g -> p g t"))
-        nc.vector.tensor_tensor(last_e[:, 3, :], halves[:, :, 0], halves[:, :, 1], ADD)
         c01, s01 = quantize(pair[:].rearrange("p k g t -> p (k g t)"), "01")
-        last_view = last_e[:].rearrange("p t g -> p g t")
-        nc.scalar.copy(fourth[:, :64], last_view[:, :64])
-        nc.vector.tensor_copy(fourth[:, 64:], last_view[:, 64:])
-        c2, s2 = quantize(third[:].rearrange("p g t -> p (g t)"), "2")
         c3, s3 = quantize(fourth[:].rearrange("p g t -> p (g t)"), "3")
+        c2, s2 = quantize(third[:].rearrange("p g t -> p (g t)"), "2")
         multiply(0, c01[:, :P], s01[:, :P])
         multiply(1, c01[:, P:], s01[:, P:])
-        multiply(2, c2[:], s2[:])
         multiply(3, c3[:], s3[:])
+        multiply(2, c2[:], s2[:])

from contextlib import ExitStack

import concourse.mybir as mybir
from concourse.masks import make_identity

F32 = mybir.dt.float32
BF16 = mybir.dt.bfloat16
U32 = mybir.dt.uint32
U16 = mybir.dt.uint16
U8 = mybir.dt.uint8
FP8X4 = mybir.dt.float8_e4m3fn_x4
MULT = mybir.AluOpType.mult
ADD = mybir.AluOpType.add

P = 128
T = 4096
D = 512
M = 256
G = 512
K = 4
E = G * K
PACK = 4
FLOPS = 2 * D * M * G

PIECES = ((1024, 1024), (1024, 1024), (1024, 512, 512), (512, 512, 512, 512))


def tile_attend_grid_kernel(tc, xT, w, part, offs, out):
    nc = tc.nc
    x_planes = xT.rearrange("(p t) c -> p t c", t=PACK)
    with ExitStack() as ctx:
        held = ctx.enter_context(tc.tile_pool(name="held", bufs=1))
        ring = ctx.enter_context(tc.tile_pool(name="ring", bufs=4))
        wide = ctx.enter_context(tc.tile_pool(name="wide", bufs=3))
        psum = ctx.enter_context(tc.psum_pool(name="psum", bufs=1))

        offsets = held.tile([P, E // 16], U16, name="offsets")
        nc.sync.dma_start(offsets[:], offs)
        part_col = held.tile([P, E // P], F32, name="part_col")
        nc.scalar.dma_start(part_col[:], part[0:1, :].rearrange("o (q i) -> (o q) i", i=E // P))
        planes = []
        for t in range(PACK):
            plane = held.tile([P, T], F32, name=f"plane{t}")
            for h in range(2):
                cols = slice(h * T // 2, (h + 1) * T // 2)
                nc.sync.dma_start(plane[:, cols], x_planes[:, t, cols])
            planes.append(plane)
        w_raw = held.tile([P, PACK, M], F32, name="w_raw")
        nc.sync.dma_start(w_raw[:], w.rearrange("(p t) m -> p t m", t=PACK))

        ident = held.tile([P, P], F32, name="ident")
        make_identity(nc, ident[:])

        part_rep = held.tile([P, E], F32, name="part_rep")
        part_view = part_rep[:].rearrange("p (q i) -> p q i", i=E // P)
        for b in range(4):
            bank = psum.tile([P, 4, P], F32, name=f"part_bank{b}", tag=f"back{b}")
            for i in range(4):
                col = part_col[:, 4 * b + i : 4 * b + i + 1]
                nc.tensor.transpose(bank[:, i, :], col.to_broadcast([P, P]), ident[:])
            src = bank[:].rearrange("p i q -> p q i")
            dst = part_view[:, :, 4 * b : 4 * b + 4]
            if b % 2 == 0:
                nc.vector.tensor_copy(dst, src)
            else:
                nc.scalar.copy(dst, src)

        sums = [psum.tile([P, PACK, P], F32, name=f"sums{k}", tag=f"fore{k}") for k in range(4)]
        backs = [psum.tile([P, PACK, P], F32, name=f"backs{k}", tag=f"back{k}") for k in range(4)]

        w_grouped = held.tile([P, M, PACK], BF16, name="w_grouped", align_bytes=64)
        w_codes = held.tile([P, M], U32, name="w_codes", align_bytes=64)
        w_scales = held.tile([P, M], U8, name="w_scales", align_bytes=64)
        last_e = held.tile([P, PACK, P], F32, name="last_e")
        nc.gpsimd.memset(last_e[:, 3, :], 0.0)
        fourth = held.tile([P, P, PACK], BF16, name="fourth", align_bytes=64)

        def sum_corners(relaid, t, k):
            for j in range(K):
                nc.tensor.matmul(
                    sums[k][:, t, :], relaid[:, j, :], ident[:], start=(j == 0), stop=(j == K - 1), is_transpose=True
                )
            turned = ring.tile([P, P], F32, name="turned")
            nc.scalar.copy(turned[:], sums[k][:, t, :])
            return turned, t, k

        def turn_back(turned, t, k):
            nc.tensor.transpose(backs[k][:, t, :], turned[:], ident[:])
            if (t, k) == (2, 3):
                nc.scalar.copy(last_e[:, 0:3, :], backs[3][:, 0:3, :])
                nc.scalar.copy(fourth[:], last_e[:].rearrange("p t g -> p g t"))

        waiting = []
        for t in range(PACK):
            e0 = 0
            for piece in PIECES[t]:
                prod = wide.tile([P, piece], F32, name=f"prod_{piece}")
                nc.vector.tensor_tensor(
                    prod[:],
                    planes[t][:].indirect(offsets[:, e0 // 16 : (e0 + piece) // 16]),
                    part_rep[:, e0 : e0 + piece],
                    MULT,
                )
                for c in range(piece // 512):
                    k = e0 // 512 + c
                    if t == 3 and k == 3:
                        continue
                    waiting.append(
                        sum_corners(prod[:, c * 512 : (c + 1) * 512].rearrange("p (g j) -> p j g", j=K), t, k)
                    )
                    if len(waiting) > 1:
                        turn_back(*waiting.pop(0))
                    if (t, k) == (3, 0):
                        nc.scalar.copy(w_grouped[:], w_raw[:].rearrange("p t m -> p m t"))
                e0 += piece
        turn_back(*waiting.pop(0))

        pair = held.tile([P, 2, P, PACK], BF16, name="pair", align_bytes=64)
        third = held.tile([P, P, PACK], BF16, name="third", align_bytes=64)

        def quantize(flat, name):
            n = flat.shape[1] // PACK
            codes = held.tile([P, n], U32, name=f"codes{name}", align_bytes=64)
            scales = held.tile([P, n], U8, name=f"scales{name}", align_bytes=64)
            nc.vector.quantize_mx(out=codes[:].bitcast(FP8X4), scales=scales[:], in_=flat)
            return codes, scales

        def multiply(k, codes, scales):
            acc = psum.tile([P, 2, P], F32, name=f"acc{k}", tag=f"fore{k}")
            for m in range(2):
                cols = slice(m * P, (m + 1) * P)
                nc.tensor.matmul_mx(
                    out=acc[:, m, :],
                    lhsT=w_codes[:, cols].bitcast(FP8X4),
                    lhsT_scale=w_scales[:, cols],
                    rhs=codes.bitcast(FP8X4),
                    rhs_scale=scales,
                    start=True,
                    stop=True,
                )
            result = held.tile([P, 2, P], F32, name=f"result{k}")
            if k < 2:
                nc.scalar.copy(result[:], acc[:])
            elif k == 3:
                nc.vector.tensor_copy(result[:], acc[:])
            else:
                nc.scalar.copy(result[:, 0, :], acc[:, 0, :])
                nc.vector.tensor_copy(result[:, 1, :], acc[:, 1, :])
            nc.sync.dma_start(out[:, k * P : (k + 1) * P].rearrange("(m p) g -> p m g", m=2), result[:])

        with nc.allow_low_precision(reason="the float32 sum of four products is rounded to bfloat16 once, on the way out"):
            nc.vector.tensor_reduce(
                fourth[:, :, 3], prod[:].rearrange("p (g j) -> p g j", j=K), mybir.AxisListType.X, ADD
            )
        nc.vector.quantize_mx(
            out=w_codes[:].bitcast(FP8X4), scales=w_scales[:], in_=w_grouped[:].rearrange("p m t -> p (m t)")
        )
        for k in range(2):
            nc.scalar.copy(pair[:, k], backs[k][:].rearrange("p t g -> p g t"))
        nc.scalar.copy(third[:], backs[2][:].rearrange("p t g -> p g t"))
        c01, s01 = quantize(pair[:].rearrange("p k g t -> p (k g t)"), "01")
        c3, s3 = quantize(fourth[:].rearrange("p g t -> p (g t)"), "3")
        c2, s2 = quantize(third[:].rearrange("p g t -> p (g t)"), "2")
        multiply(0, c01[:, :P], s01[:, :P])
        multiply(1, c01[:, P:], s01[:, P:])
        multiply(3, c3[:], s3[:])
        multiply(2, c2[:], s2[:])
